import numpy as np
import ml_dtypes


def mxq(x, axis, fmt="e4m3"):
    dtype, down = {"e4m3": (ml_dtypes.float8_e4m3fn, 7), "e5m2": (ml_dtypes.float8_e5m2, 14)}[fmt]
    v = np.moveaxis(np.asarray(x, np.float32).astype(ml_dtypes.bfloat16).astype(np.float64), axis, -1)
    blocks = v.reshape(v.shape[:-1] + (-1, 32))
    amax = np.abs(blocks).max(-1, keepdims=True)
    byte = np.maximum(np.where(amax > 0, np.frexp(amax)[1] - 1 + 127, 0) - down, 1)
    scale = np.exp2(byte - 127.0)
    codes = (blocks / scale).astype(np.float32).astype(dtype).astype(np.float64)
    return np.moveaxis((codes * scale).reshape(v.shape), -1, axis)


WIDE = False


def mx_kscale(k):
    if not WIDE:
        return np.ones(k)
    levels = np.array([10, -10, 5, -5, 0])
    if k % 512:
        return np.exp2(np.random.permutation(np.resize(levels, k // 32))).repeat(32)
    a = np.empty((k // 512, 16))
    for p in range(k // 512):
        a[p, :8] = np.random.permutation(np.resize(levels, 8))
        for g in range(8):
            far = levels[np.abs(levels - a[p, g]) >= 10]
            a[p, g + 8] = far[np.random.randint(len(far))]
    return np.exp2(a.ravel()).repeat(32)


def f64(x):
    return np.asarray(x).astype(np.float64)


def striped(idx):
    return np.tile(idx.reshape(-1, 16).T, (8, 1)).astype(np.uint16)


def unstriped(offs):
    return offs[:16].T.reshape(-1).astype(np.int64)


def striped8(idx):
    return np.concatenate([x.reshape(-1, 16).T for x in idx]).astype(np.uint16)


def runs(offs, k):
    lists = np.stack([offs[16 * r : 16 * r + 16].T.reshape(-1) for r in range(8)]).astype(np.int64)
    return lists[np.arange(k) % 512 // 64]


def pack_weight(w):
    k, n = w.shape
    w = f64(np.asarray(w, np.float32).astype(ml_dtypes.bfloat16)).reshape(k // 32, 32, n)
    amax = np.abs(w).max(1)
    byte = np.clip(np.where(amax > 0, np.frexp(amax)[1] - 1 + 127 - 7, 1), 1, 254)
    scaled = (w * np.exp2(127.0 - byte)[:, None, :]).reshape(k, n).astype(np.float32)
    words = np.ascontiguousarray(scaled.reshape(k // 512, 128, 4, n).transpose(0, 1, 3, 2)).astype(ml_dtypes.float8_e4m3fn).view(np.uint8)
    return words, np.ascontiguousarray(byte.astype(np.uint8).reshape(k // 512, 16, n))


def unpack_weight(words, scales):
    g, p, n, _ = words.shape
    vals = np.ascontiguousarray(words).view(ml_dtypes.float8_e4m3fn).astype(np.float64) * np.repeat(np.exp2(scales.astype(np.float64) - 127.0), 8, axis=1)[..., None]
    return vals.transpose(0, 1, 3, 2).reshape(g * 512, n)


def relu(v):
    return np.maximum(v, 0.0)


K, T, S, H, C = 512, 2048, 512, 512, 512


def setup_inputs():
    n = np.random.standard_normal
    s = mx_kscale(K)[:, None]
    packed_xT = pack_weight(n((K, T)) * s)
    return {
        "x_words": packed_xT[0],
        "x_scales": packed_xT[1],
        "w1": (n((K, H)) / np.sqrt(K) / s).astype(np.float32),
        "gs": (np.random.uniform(0.5, 1.5, (K, 1)) / s).astype(np.float32),
        "offs": striped(np.random.permutation(T)[:S]),
        "cand": striped(np.random.permutation(T)[:C]),
        "n1": striped8(np.stack([np.random.permutation(S) for _ in range(8)])),
        "n2": striped8(np.stack([np.random.permutation(S) for _ in range(8)])),
    }


def reference(x_words, x_scales, w1, gs, offs, cand, n1, n2):
    x_cand = unpack_weight(x_words, x_scales)[:, unstriped(cand)]
    xq = unpack_weight(x_words, x_scales)[:, unstriped(offs)]
    h = relu(mxq(f64(w1), 0, "e4m3").T @ xq)
    z = f64(gs) * h
    s = 0.0625 * ((x_cand.T @ mxq(z, 0, "e4m3")))
    a = s[np.arange(C)[:, None], runs(n1, C)]
    b = s[np.arange(C)[:, None], runs(n2, C)]
    return s - (np.maximum(np.minimum(s, a), np.minimum(np.maximum(s, a), b)))

@@ -1,0 +1,189 @@
+from contextlib import ExitStack
+
+import concourse.mybir as mybir
+
+K, T, S, H, C = 512, 2048, 512, 512, 512
+FLOPS = 2 * K * H * S + 2 * K * C * S
+
+F32 = mybir.dt.float32
+BF16 = mybir.dt.bfloat16
+I32 = mybir.dt.int32
+U32 = mybir.dt.uint32
+U16 = mybir.dt.uint16
+U8 = mybir.dt.uint8
+FP8X4 = mybir.dt.float8_e4m3fn_x4
+ALU = mybir.AluOpType
+ACT = mybir.ActivationFunctionType
+
+P = 128
+PACK = 4
+BLK = 128
+NBLK = S // BLK
+HALF = 64
+
+
+def tile_picked_candmed_none_p_kernel(tc, x_words, x_scales, w1, gs, offs, cand, n1, n2, out):
+    nc = tc.nc
+    with ExitStack() as ctx:
+        held = ctx.enter_context(tc.tile_pool(name="held", bufs=1))
+        psum = ctx.enter_context(tc.psum_pool(name="psum", bufs=1))
+
+        offs_t = held.tile([P, S // 16], U16, name="offs_t")
+        cand_t = held.tile([P, C // 16], U16, name="cand_t")
+        n1_t = held.tile([P, S // 16], U16, name="n1_t")
+        n2_t = held.tile([P, S // 16], U16, name="n2_t")
+        xw = held.tile([P, T], I32, name="xw", align_bytes=64)
+        xs = held.tile([P, T], U8, name="xs", align_bytes=64)
+        gs_t = held.tile([P, 1, PACK], F32, name="gs_t")
+        w_raw = [held.tile([P, PACK, H // 2], F32, name="w_raw%d" % h) for h in range(2)]
+
+        nc.vector.memset(xs[:].bitcast(I32), 0)
+        nc.sync.dma_start(offs_t[:], offs)
+        nc.sync.dma_start(cand_t[:], cand)
+        nc.scalar.dma_start(xs[0:16, :].bitcast(I32), x_scales[0].bitcast(I32))
+        nc.sync.dma_start(xw[:], x_words[0].rearrange("p n t -> p (n t)").bitcast(I32))
+        nc.sync.dma_start(n1_t[:], n1)
+        nc.sync.dma_start(n2_t[:], n2)
+        w_view = w1.rearrange("(p j) c -> p j c", j=PACK)
+        for h in range(2):
+            nc.sync.dma_start(w_raw[h][:], w_view[:, :, h * (H // 2) : (h + 1) * (H // 2)])
+        nc.gpsimd.dma_start(gs_t[:], gs.rearrange("(p t) o -> p o t", t=PACK))
+
+        xq_w = held.tile([P, S], U32, name="xq_w", align_bytes=64)
+        picked_s = held.tile([P, S + C], U8, name="picked_s", align_bytes=64)
+        placed_s = held.tile([P, S + C], U8, name="placed_s", align_bytes=64)
+        nc.vector.memset(placed_s[:].bitcast(I32), 0)
+        xc_w_list = held.tile([P, C], U32, name="xc_w_list", align_bytes=64)
+
+        nc.vector.tensor_copy(picked_s[:, 0:S], xs[:].indirect(offs_t[:]))
+        nc.vector.tensor_copy(picked_s[:, S : S + C], xs[:].indirect(cand_t[:]))
+        for q in range(4):
+            nc.sync.dma_start(placed_s[32 * q : 32 * q + 4, :].bitcast(I32), picked_s[4 * q : 4 * q + 4, :].bitcast(I32))
+        nc.vector.tensor_copy(xq_w[:], xw[:].bitcast(U32).indirect(offs_t[:]))
+        nc.vector.tensor_copy(xc_w_list[:], xw[:].bitcast(U32).indirect(cand_t[:]))
+        xc_w_by_t = xc_w_list[:].rearrange("p (m t) -> p m t", t=PACK)
+
+        wq_w = held.tile([P, H], U32, name="wq_w", align_bytes=64)
+        wq_s = held.tile([P, H], U8, name="wq_s", align_bytes=64)
+        for h in range(2):
+            w_bf = held.tile([P, PACK, HALF, PACK], BF16, name="w_bf%d" % h, tag="w_bf%d" % h, align_bytes=64)
+            nc.scalar.copy(
+                w_bf[:].rearrange("p t m j -> p m j t"), w_raw[h][:].rearrange("p j (m t) -> p m j t", t=PACK)
+            )
+            for t in range(PACK):
+                cols = slice(P * t + HALF * h, P * t + HALF * (h + 1))
+                nc.vector.quantize_mx(
+                    out=wq_w[:, cols].bitcast(FP8X4),
+                    scales=wq_s[:, cols],
+                    in_=w_bf[:, t, :, :].rearrange("p m j -> p (m j)"),
+                )
+
+        xc_s = held.tile([P, C], U8, name="xc_s", tag="w_bf1", align_bytes=64)
+        nc.vector.tensor_copy(
+            xc_s[:].rearrange("p (t m) -> p t m", t=PACK),
+            placed_s[:, S : S + C].rearrange("p (m t) -> p t m", t=PACK),
+        )
+
+        xc_w_first = held.tile([P, P], U32, name="xc_w_first", tag="w_bf0", align_bytes=64)
+        nc.vector.tensor_copy(xc_w_first[:], xc_w_by_t[:, :, 0])
+
+        zq_w = held.tile([P, S], U32, name="zq_w", align_bytes=64)
+        zq_s = held.tile([P, S], U8, name="zq_s", align_bytes=64)
+        z_bf = [held.tile([P, BLK, PACK], BF16, name="z_bf%d" % u, tag="z_bf%d" % u, align_bytes=64) for u in range(NBLK)]
+
+        def first_product(u):
+            cols = slice(BLK * u, BLK * (u + 1))
+            h_ps = psum.tile([P, PACK, BLK], F32, name="h_ps", tag="bank%d" % u)
+            for t in range(PACK):
+                feats = slice(P * t, P * (t + 1))
+                nc.tensor.matmul_mx(
+                    out=h_ps[:, t, :],
+                    lhsT=wq_w[:, feats].bitcast(FP8X4),
+                    lhsT_scale=wq_s[:, feats],
+                    rhs=xq_w[:, cols].bitcast(FP8X4),
+                    rhs_scale=placed_s[:, cols],
+                    start=True,
+                    stop=True,
+                )
+            nc.vector.scalar_tensor_tensor(
+                out=z_bf[u][:],
+                in0=h_ps[:].rearrange("p t n -> p n t"),
+                scalar=0.0,
+                in1=gs_t[:].to_broadcast([P, BLK, PACK]),
+                op0=ALU.max,
+                op1=ALU.mult,
+            )
+
+        def quantise_z(u):
+            cols = slice(BLK * u, BLK * (u + 1))
+            nc.vector.quantize_mx(
+                out=zq_w[:, cols].bitcast(FP8X4), scales=zq_s[:, cols], in_=z_bf[u][:].rearrange("p n t -> p (n t)")
+            )
+
+        window = [held.tile([P, 2 * S], F32, name="window%d" % t) for t in range(PACK)]
+        own = [held.tile([P, S], F32, name="own%d" % t) for t in range(PACK)]
+
+        def second_product(t, lo, hi, bank, words):
+            rows = slice(P * t, P * (t + 1))
+            s_ps = psum.tile([P, hi - lo], F32, name="s_ps", tag="bank%d" % bank)
+            nc.tensor.matmul_mx(
+                out=s_ps[:],
+                lhsT=words.bitcast(FP8X4),
+                lhsT_scale=xc_s[:, rows],
+                rhs=zq_w[:, lo:hi].bitcast(FP8X4),
+                rhs_scale=zq_s[:, lo:hi],
+                start=True,
+                stop=True,
+            )
+            nc.scalar.activation(window[t][:, lo:hi], s_ps[:], ACT.Copy, scale=-0.0625)
+            nc.scalar.activation(own[t][:, lo:hi], s_ps[:], ACT.Copy, scale=-0.0625)
+
+        first_product(0)
+        first_product(1)
+        quantise_z(0)
+        first_product(2)
+        quantise_z(1)
+        second_product(0, 0, 2 * BLK, 4, xc_w_first[:])
+        first_product(3)
+        quantise_z(2)
+        second_product(0, 2 * BLK, 3 * BLK, 0, xc_w_first[:])
+        quantise_z(3)
+        second_product(0, 3 * BLK, 4 * BLK, 1, xc_w_first[:])
+        xc_w_rest = held.tile([P, PACK - 1, P], U32, name="xc_w_rest", tag="z_bf3", align_bytes=64)
+        nc.vector.tensor_copy(xc_w_rest[:].rearrange("p t m -> p m t"), xc_w_by_t[:, :, 1:PACK])
+        for t in range(1, PACK):
+            second_product(t, 0, S, 4 + t, xc_w_rest[:, t - 1, :])
+
+        da = [held.tile([P, S], F32, name="da%d" % t) for t in range(PACK)]
+        db = [held.tile([P, S], F32, name="db%d" % t) for t in range(PACK)]
+        low = [held.tile([P, S], F32, name="low%d" % t) for t in range(PACK)]
+        res = [held.tile([P, S], F32, name="res%d" % t) for t in range(PACK)]
+        out_view = out.rearrange("(p t) j -> p t j", t=PACK)
+
+        def fetch(dst, lists, t):
+            nc.vector.tensor_tensor(dst[t][:], window[t][:].indirect(lists[:]), own[t][:], ALU.subtract)
+
+        def clamp_low(t, cols):
+            nc.vector.scalar_tensor_tensor(
+                out=low[t][:, cols], in0=db[t][:, cols], scalar=0.0, in1=da[t][:, cols], op0=ALU.min, op1=ALU.max
+            )
+
+        def clamp_high(t, cols):
+            nc.vector.scalar_tensor_tensor(
+                out=res[t][:, cols], in0=db[t][:, cols], scalar=0.0, in1=low[t][:, cols], op0=ALU.max, op1=ALU.min
+            )
+            nc.sync.dma_start(out_view[:, t, cols], res[t][:, cols])
+
+        whole = slice(0, S)
+        fetch(da, n1_t, 0)
+        fetch(db, n2_t, 0)
+        for t in range(1, PACK):
+            fetch(da, n1_t, t)
+            clamp_low(t - 1, whole)
+            fetch(db, n2_t, t)
+            clamp_high(t - 1, whole)
+        halves = [slice(0, S // 2), slice(S // 2, S)]
+        for cols in halves:
+            clamp_low(PACK - 1, cols)
+        for cols in halves:
+            clamp_high(PACK - 1, cols)

@@ -37,17 +37,18 @@ def tile_picked_candmed_none_p_kernel(tc, x_words, x_scales, w1, gs, offs, cand,
         gs_t = held.tile([P, 1, PACK], F32, name="gs_t")
         w_raw = [held.tile([P, PACK, H // 2], F32, name="w_raw%d" % h) for h in range(2)]
 
-        nc.vector.memset(xs[:].bitcast(I32), 0)
+        for lo, hi in ((0, 16), (32, 64), (64, 128)):
+            nc.vector.memset(xs[lo:hi, :].bitcast(I32), 0)
         nc.sync.dma_start(offs_t[:], offs)
+        nc.sync.dma_start(xs[16:32, :].bitcast(I32), x_scales[0].bitcast(I32))
         nc.sync.dma_start(cand_t[:], cand)
-        nc.scalar.dma_start(xs[0:16, :].bitcast(I32), x_scales[0].bitcast(I32))
         nc.sync.dma_start(xw[:], x_words[0].rearrange("p n t -> p (n t)").bitcast(I32))
         nc.sync.dma_start(n1_t[:], n1)
-        nc.sync.dma_start(n2_t[:], n2)
         w_view = w1.rearrange("(p j) c -> p j c", j=PACK)
         for h in range(2):
             nc.sync.dma_start(w_raw[h][:], w_view[:, :, h * (H // 2) : (h + 1) * (H // 2)])
-        nc.gpsimd.dma_start(gs_t[:], gs.rearrange("(p t) o -> p o t", t=PACK))
+        nc.sync.dma_start(gs_t[:], gs.rearrange("(p t) o -> p o t", t=PACK))
+        nc.sync.dma_start(n2_t[:], n2)
 
         xq_w = held.tile([P, S], U32, name="xq_w", align_bytes=64)
         picked_s = held.tile([P, S + C], U8, name="picked_s", align_bytes=64)
@@ -58,38 +59,47 @@ def tile_picked_candmed_none_p_kernel(tc, x_words, x_scales, w1, gs, offs, cand,
         nc.vector.tensor_copy(picked_s[:, 0:S], xs[:].indirect(offs_t[:]))
         nc.vector.tensor_copy(picked_s[:, S : S + C], xs[:].indirect(cand_t[:]))
         for q in range(4):
-            nc.sync.dma_start(placed_s[32 * q : 32 * q + 4, :].bitcast(I32), picked_s[4 * q : 4 * q + 4, :].bitcast(I32))
+            nc.sync.dma_start(placed_s[32 * q : 32 * q + 4, :].bitcast(I32), picked_s[16 + 4 * q : 20 + 4 * q, :].bitcast(I32))
         nc.vector.tensor_copy(xq_w[:], xw[:].bitcast(U32).indirect(offs_t[:]))
         nc.vector.tensor_copy(xc_w_list[:], xw[:].bitcast(U32).indirect(cand_t[:]))
         xc_w_by_t = xc_w_list[:].rearrange("p (m t) -> p m t", t=PACK)
 
         wq_w = held.tile([P, H], U32, name="wq_w", align_bytes=64)
         wq_s = held.tile([P, H], U8, name="wq_s", align_bytes=64)
-        for h in range(2):
-            w_bf = held.tile([P, PACK, HALF, PACK], BF16, name="w_bf%d" % h, tag="w_bf%d" % h, align_bytes=64)
-            nc.scalar.copy(
-                w_bf[:].rearrange("p t m j -> p m j t"), w_raw[h][:].rearrange("p j (m t) -> p m j t", t=PACK)
+        w_bf = [
+            held.tile([P, 2, P, PACK], BF16, name="w_bf%d" % g, tag="w_bf%d" % g, align_bytes=64) for g in range(2)
+        ]
+
+        def cast_weights(copy, h, g):
+            copy(
+                w_bf[g][:, :, HALF * h : HALF * (h + 1), :].rearrange("p t m j -> p m j t"),
+                w_raw[h][:].rearrange("p j (m t) -> p m j t", t=PACK)[:, :, :, 2 * g : 2 * g + 2],
             )
-            for t in range(PACK):
-                cols = slice(P * t + HALF * h, P * t + HALF * (h + 1))
-                nc.vector.quantize_mx(
-                    out=wq_w[:, cols].bitcast(FP8X4),
-                    scales=wq_s[:, cols],
-                    in_=w_bf[:, t, :, :].rearrange("p m j -> p (m j)"),
-                )
 
-        xc_s = held.tile([P, C], U8, name="xc_s", tag="w_bf1", align_bytes=64)
-        nc.vector.tensor_copy(
-            xc_s[:].rearrange("p (t m) -> p t m", t=PACK),
-            placed_s[:, S : S + C].rearrange("p (m t) -> p t m", t=PACK),
-        )
+        cast_weights(nc.scalar.copy, 0, 1)
+        cast_weights(nc.scalar.copy, 0, 0)
+        cast_weights(nc.scalar.copy, 1, 0)
+        cast_weights(nc.vector.tensor_copy, 1, 1)
+        for g in range(2):
+            cols = slice(2 * P * g, 2 * P * (g + 1))
+            nc.vector.quantize_mx(
+                out=wq_w[:, cols].bitcast(FP8X4), scales=wq_s[:, cols], in_=w_bf[g][:].rearrange("p t m j -> p (t m j)")
+            )
 
-        xc_w_first = held.tile([P, P], U32, name="xc_w_first", tag="w_bf0", align_bytes=64)
+        xc_s_by_t = placed_s[:, S : S + C].rearrange("p (m t) -> p t m", t=PACK)
+        xc_s_first = held.tile([P, P], U8, name="xc_s_first", tag="w_bf0", align_bytes=64)
+        nc.vector.tensor_copy(xc_s_first[:], xc_s_by_t[:, 0, :])
+        xc_w_first = held.tile([P, P], U32, name="xc_w_first", tag="w_bf1", align_bytes=64)
         nc.vector.tensor_copy(xc_w_first[:], xc_w_by_t[:, :, 0])
 
         zq_w = held.tile([P, S], U32, name="zq_w", align_bytes=64)
         zq_s = held.tile([P, S], U8, name="zq_s", align_bytes=64)
-        z_bf = [held.tile([P, BLK, PACK], BF16, name="z_bf%d" % u, tag="z_bf%d" % u, align_bytes=64) for u in range(NBLK)]
+        z_spans = [(0, 2 * BLK), (2 * BLK, 3 * BLK), (3 * BLK, S)]
+        z_tiles = [
+            held.tile([P, hi - lo, PACK], BF16, name="z_bf%d" % i, tag="z_bf%d" % i, align_bytes=64)
+            for i, (lo, hi) in enumerate(z_spans)
+        ]
+        z_bf = [z_tiles[0][:, 0:BLK, :], z_tiles[0][:, BLK : 2 * BLK, :], z_tiles[1][:], z_tiles[2][:]]
 
         def first_product(u):
             cols = slice(BLK * u, BLK * (u + 1))
@@ -106,7 +116,7 @@ def tile_picked_candmed_none_p_kernel(tc, x_words, x_scales, w1, gs, offs, cand,
                     stop=True,
                 )
             nc.vector.scalar_tensor_tensor(
-                out=z_bf[u][:],
+                out=z_bf[u],
                 in0=h_ps[:].rearrange("p t n -> p n t"),
                 scalar=0.0,
                 in1=gs_t[:].to_broadcast([P, BLK, PACK]),
@@ -114,22 +124,21 @@ def tile_picked_candmed_none_p_kernel(tc, x_words, x_scales, w1, gs, offs, cand,
                 op1=ALU.mult,
             )
 
-        def quantise_z(u):
-            cols = slice(BLK * u, BLK * (u + 1))
+        def quantise_z(i):
+            cols = slice(*z_spans[i])
             nc.vector.quantize_mx(
-                out=zq_w[:, cols].bitcast(FP8X4), scales=zq_s[:, cols], in_=z_bf[u][:].rearrange("p n t -> p (n t)")
+                out=zq_w[:, cols].bitcast(FP8X4), scales=zq_s[:, cols], in_=z_tiles[i][:].rearrange("p n t -> p (n t)")
             )
 
         window = [held.tile([P, 2 * S], F32, name="window%d" % t) for t in range(PACK)]
         own = [held.tile([P, S], F32, name="own%d" % t) for t in range(PACK)]
 
-        def second_product(t, lo, hi, bank, words):
-            rows = slice(P * t, P * (t + 1))
+        def second_product(t, lo, hi, bank, words, scales):
             s_ps = psum.tile([P, hi - lo], F32, name="s_ps", tag="bank%d" % bank)
             nc.tensor.matmul_mx(
                 out=s_ps[:],
                 lhsT=words.bitcast(FP8X4),
-                lhsT_scale=xc_s[:, rows],
+                lhsT_scale=scales,
                 rhs=zq_w[:, lo:hi].bitcast(FP8X4),
                 rhs_scale=zq_s[:, lo:hi],
                 start=True,
@@ -140,19 +149,20 @@ def tile_picked_candmed_none_p_kernel(tc, x_words, x_scales, w1, gs, offs, cand,
 
         first_product(0)
         first_product(1)
-        quantise_z(0)
         first_product(2)
+        quantise_z(0)
+        second_product(0, 0, 2 * BLK, 4, xc_w_first[:], xc_s_first[:])
         quantise_z(1)
-        second_product(0, 0, 2 * BLK, 4, xc_w_first[:])
+        second_product(0, 2 * BLK, 3 * BLK, 0, xc_w_first[:], xc_s_first[:])
         first_product(3)
+        xc_s_rest = held.tile([P, PACK - 1, P], U8, name="xc_s_rest", tag="z_bf1", align_bytes=64)
+        nc.vector.tensor_copy(xc_s_rest[:], xc_s_by_t[:, 1:PACK, :])
         quantise_z(2)
-        second_product(0, 2 * BLK, 3 * BLK, 0, xc_w_first[:])
-        quantise_z(3)
-        second_product(0, 3 * BLK, 4 * BLK, 1, xc_w_first[:])
-        xc_w_rest = held.tile([P, PACK - 1, P], U32, name="xc_w_rest", tag="z_bf3", align_bytes=64)
+        second_product(0, 3 * BLK, 4 * BLK, 1, xc_w_first[:], xc_s_first[:])
+        xc_w_rest = held.tile([P, PACK - 1, P], U32, name="xc_w_rest", tag="z_bf2", align_bytes=64)
         nc.vector.tensor_copy(xc_w_rest[:].rearrange("p t m -> p m t"), xc_w_by_t[:, :, 1:PACK])
         for t in range(1, PACK):
-            second_product(t, 0, S, 4 + t, xc_w_rest[:, t - 1, :])
+            second_product(t, 0, S, 4 + t, xc_w_rest[:, t - 1, :], xc_s_rest[:, t - 1, :])
 
         da = [held.tile([P, S], F32, name="da%d" % t) for t in range(PACK)]
         db = [held.tile([P, S], F32, name="db%d" % t) for t in range(PACK)]
@@ -160,8 +170,9 @@ def tile_picked_candmed_none_p_kernel(tc, x_words, x_scales, w1, gs, offs, cand,
         res = [held.tile([P, S], F32, name="res%d" % t) for t in range(PACK)]
         out_view = out.rearrange("(p t) j -> p t j", t=PACK)
 
-        def fetch(dst, lists, t):
-            nc.vector.tensor_tensor(dst[t][:], window[t][:].indirect(lists[:]), own[t][:], ALU.subtract)
+        def fetch(dst, lists, t, cols):
+            offsets = lists[:, cols.start // 16 : cols.stop // 16]
+            nc.vector.tensor_tensor(dst[t][:, cols], window[t][:].indirect(offsets), own[t][:, cols], ALU.subtract)
 
         def clamp_low(t, cols):
             nc.vector.scalar_tensor_tensor(
@@ -175,14 +186,15 @@ def tile_picked_candmed_none_p_kernel(tc, x_words, x_scales, w1, gs, offs, cand,
             nc.sync.dma_start(out_view[:, t, cols], res[t][:, cols])
 
         whole = slice(0, S)
-        fetch(da, n1_t, 0)
-        fetch(db, n2_t, 0)
-        for t in range(1, PACK):
-            fetch(da, n1_t, t)
-            clamp_low(t - 1, whole)
-            fetch(db, n2_t, t)
-            clamp_high(t - 1, whole)
         halves = [slice(0, S // 2), slice(S // 2, S)]
+        for cols in halves:
+            fetch(da, n1_t, 0, cols)
+        fetch(db, n2_t, 0, whole)
+        for t in range(1, PACK):
+            fetch(da, n1_t, t, whole)
+            clamp_low(t - 1, whole)
+            fetch(db, n2_t, t, whole)
+            clamp_high(t - 1, whole)
         for cols in halves:
             clamp_low(PACK - 1, cols)
         for cols in halves:

@@ -80,7 +80,7 @@ def tile_picked_candmed_none_p_kernel(tc, x_words, x_scales, w1, gs, offs, cand,
         cast_weights(nc.scalar.copy, 0, 0)
         cast_weights(nc.scalar.copy, 1, 0)
         cast_weights(nc.vector.tensor_copy, 1, 1)
-        for g in range(2):
+        for g in (1, 0):
             cols = slice(2 * P * g, 2 * P * (g + 1))
             nc.vector.quantize_mx(
                 out=wq_w[:, cols].bitcast(FP8X4), scales=wq_s[:, cols], in_=w_bf[g][:].rearrange("p t m j -> p (t m j)")
@@ -104,7 +104,7 @@ def tile_picked_candmed_none_p_kernel(tc, x_words, x_scales, w1, gs, offs, cand,
         def first_product(u):
             cols = slice(BLK * u, BLK * (u + 1))
             h_ps = psum.tile([P, PACK, BLK], F32, name="h_ps", tag="bank%d" % u)
-            for t in range(PACK):
+            for t in (2, 3, 0, 1):
                 feats = slice(P * t, P * (t + 1))
                 nc.tensor.matmul_mx(
                     out=h_ps[:, t, :],
@@ -183,19 +183,19 @@ def tile_picked_candmed_none_p_kernel(tc, x_words, x_scales, w1, gs, offs, cand,
             nc.vector.scalar_tensor_tensor(
                 out=res[t][:, cols], in0=db[t][:, cols], scalar=0.0, in1=low[t][:, cols], op0=ALU.max, op1=ALU.min
             )
-            nc.sync.dma_start(out_view[:, t, cols], res[t][:, cols])
+            if t == PACK - 1:
+                nc.sync.dma_start(out_view[:, t, cols], res[t][:, cols])
 
         whole = slice(0, S)
         halves = [slice(0, S // 2), slice(S // 2, S)]
-        for cols in halves:
-            fetch(da, n1_t, 0, cols)
-        fetch(db, n2_t, 0, whole)
-        for t in range(1, PACK):
-            fetch(da, n1_t, t, whole)
-            clamp_low(t - 1, whole)
-            fetch(db, n2_t, t, whole)
-            clamp_high(t - 1, whole)
-        for cols in halves:
-            clamp_low(PACK - 1, cols)
-        for cols in halves:
-            clamp_high(PACK - 1, cols)
+        for t in range(PACK):
+            for cols in halves if t == 0 else [whole]:
+                fetch(da, n1_t, t, cols)
+            for cols in halves:
+                fetch(db, n2_t, t, cols)
+            for cols in halves:
+                clamp_low(t, cols)
+            for cols in halves:
+                clamp_high(t, cols)
+            if t < PACK - 1:
+                nc.sync.dma_start(out_view[:, t, :], res[t][:])

@@ -42,12 +42,12 @@ def tile_picked_candmed_none_p_kernel(tc, x_words, x_scales, w1, gs, offs, cand,
         nc.sync.dma_start(offs_t[:], offs)
         nc.sync.dma_start(xs[16:32, :].bitcast(I32), x_scales[0].bitcast(I32))
         nc.sync.dma_start(cand_t[:], cand)
+        nc.scalar.dma_start(gs_t[:], gs.rearrange("(p t) o -> p o t", t=PACK))
         nc.sync.dma_start(xw[:], x_words[0].rearrange("p n t -> p (n t)").bitcast(I32))
-        nc.sync.dma_start(n1_t[:], n1)
         w_view = w1.rearrange("(p j) c -> p j c", j=PACK)
         for h in range(2):
             nc.sync.dma_start(w_raw[h][:], w_view[:, :, h * (H // 2) : (h + 1) * (H // 2)])
-        nc.sync.dma_start(gs_t[:], gs.rearrange("(p t) o -> p o t", t=PACK))
+        nc.sync.dma_start(n1_t[:], n1)
         nc.sync.dma_start(n2_t[:], n2)
 
         xq_w = held.tile([P, S], U32, name="xq_w", align_bytes=64)
@@ -145,24 +145,29 @@ def tile_picked_candmed_none_p_kernel(tc, x_words, x_scales, w1, gs, offs, cand,
                 stop=True,
             )
             nc.scalar.activation(window[t][:, lo:hi], s_ps[:], ACT.Copy, scale=-0.0625)
+            return s_ps
+
+        def own_copy(t, lo, hi, s_ps):
             nc.scalar.activation(own[t][:, lo:hi], s_ps[:], ACT.Copy, scale=-0.0625)
 
         first_product(0)
         first_product(1)
         first_product(2)
         quantise_z(0)
-        second_product(0, 0, 2 * BLK, 4, xc_w_first[:], xc_s_first[:])
-        quantise_z(1)
-        second_product(0, 2 * BLK, 3 * BLK, 0, xc_w_first[:], xc_s_first[:])
+        own_copy(0, 0, 2 * BLK, second_product(0, 0, 2 * BLK, 4, xc_w_first[:], xc_s_first[:]))
         first_product(3)
+        quantise_z(1)
+        third = second_product(0, 2 * BLK, 3 * BLK, 0, xc_w_first[:], xc_s_first[:])
+        quantise_z(2)
+        fourth = second_product(0, 3 * BLK, S, 1, xc_w_first[:], xc_s_first[:])
+        own_copy(0, 2 * BLK, 3 * BLK, third)
+        own_copy(0, 3 * BLK, S, fourth)
         xc_s_rest = held.tile([P, PACK - 1, P], U8, name="xc_s_rest", tag="z_bf1", align_bytes=64)
         nc.vector.tensor_copy(xc_s_rest[:], xc_s_by_t[:, 1:PACK, :])
-        quantise_z(2)
-        second_product(0, 3 * BLK, 4 * BLK, 1, xc_w_first[:], xc_s_first[:])
         xc_w_rest = held.tile([P, PACK - 1, P], U32, name="xc_w_rest", tag="z_bf2", align_bytes=64)
         nc.vector.tensor_copy(xc_w_rest[:].rearrange("p t m -> p m t"), xc_w_by_t[:, :, 1:PACK])
         for t in range(1, PACK):
-            second_product(t, 0, S, 4 + t, xc_w_rest[:, t - 1, :], xc_s_rest[:, t - 1, :])
+            own_copy(t, 0, S, second_product(t, 0, S, 4 + t, xc_w_rest[:, t - 1, :], xc_s_rest[:, t - 1, :]))
 
         da = [held.tile([P, S], F32, name="da%d" % t) for t in range(PACK)]
         db = [held.tile([P, S], F32, name="db%d" % t) for t in range(PACK)]

@@ -17,9 +17,12 @@ ACT = mybir.ActivationFunctionType
 
 P = 128
 PACK = 4
+GROUP = 16
+QUADRANT = 32
+SCALE_ROWS = K // 32
 BLK = 128
-NBLK = S // BLK
-HALF = 64
+HALF = P // 2
+NEG_SIXTEENTH = -0.0625
 
 
 def tile_picked_candmed_none_p_kernel(tc, x_words, x_scales, w1, gs, offs, cand, n1, n2, out):
@@ -28,19 +31,21 @@ def tile_picked_candmed_none_p_kernel(tc, x_words, x_scales, w1, gs, offs, cand,
         held = ctx.enter_context(tc.tile_pool(name="held", bufs=1))
         psum = ctx.enter_context(tc.psum_pool(name="psum", bufs=1))
 
-        offs_t = held.tile([P, S // 16], U16, name="offs_t")
-        cand_t = held.tile([P, C // 16], U16, name="cand_t")
-        n1_t = held.tile([P, S // 16], U16, name="n1_t")
-        n2_t = held.tile([P, S // 16], U16, name="n2_t")
+        offs_t = held.tile([P, S // GROUP], U16, name="offs_t")
+        cand_t = held.tile([P, C // GROUP], U16, name="cand_t")
+        n1_t = held.tile([P, S // GROUP], U16, name="n1_t")
+        n2_t = held.tile([P, S // GROUP], U16, name="n2_t")
         xw = held.tile([P, T], I32, name="xw", align_bytes=64)
         xs = held.tile([P, T], U8, name="xs", align_bytes=64)
         gs_t = held.tile([P, 1, PACK], F32, name="gs_t")
-        w_raw = [held.tile([P, PACK, H // 2], F32, name="w_raw%d" % h) for h in range(2)]
+        w_raw = [
+            held.tile([P, PACK, H // 2], F32, name="w_raw%d" % h, tag="w_raw%d" % h, align_bytes=64) for h in range(2)
+        ]
 
-        for lo, hi in ((0, 16), (32, 64), (64, 128)):
+        for lo, hi in ((0, SCALE_ROWS), (QUADRANT, 2 * QUADRANT), (2 * QUADRANT, P)):
             nc.vector.memset(xs[lo:hi, :].bitcast(I32), 0)
         nc.sync.dma_start(offs_t[:], offs)
-        nc.sync.dma_start(xs[16:32, :].bitcast(I32), x_scales[0].bitcast(I32))
+        nc.sync.dma_start(xs[SCALE_ROWS:QUADRANT, :].bitcast(I32), x_scales[0].bitcast(I32))
         nc.sync.dma_start(cand_t[:], cand)
         nc.scalar.dma_start(gs_t[:], gs.rearrange("(p t) o -> p o t", t=PACK))
         nc.sync.dma_start(xw[:], x_words[0].rearrange("p n t -> p (n t)").bitcast(I32))
@@ -58,8 +63,11 @@ def tile_picked_candmed_none_p_kernel(tc, x_words, x_scales, w1, gs, offs, cand,
 
         nc.vector.tensor_copy(picked_s[:, 0:S], xs[:].indirect(offs_t[:]))
         nc.vector.tensor_copy(picked_s[:, S : S + C], xs[:].indirect(cand_t[:]))
-        for q in range(4):
-            nc.sync.dma_start(placed_s[32 * q : 32 * q + 4, :].bitcast(I32), picked_s[16 + 4 * q : 20 + 4 * q, :].bitcast(I32))
+        for q in range(P // QUADRANT):
+            nc.sync.dma_start(
+                placed_s[QUADRANT * q : QUADRANT * q + PACK, :].bitcast(I32),
+                picked_s[SCALE_ROWS + PACK * q : SCALE_ROWS + PACK * (q + 1), :].bitcast(I32),
+            )
         nc.vector.tensor_copy(xq_w[:], xw[:].bitcast(U32).indirect(offs_t[:]))
         nc.vector.tensor_copy(xc_w_list[:], xw[:].bitcast(U32).indirect(cand_t[:]))
         xc_w_by_t = xc_w_list[:].rearrange("p (m t) -> p m t", t=PACK)
@@ -72,7 +80,7 @@ def tile_picked_candmed_none_p_kernel(tc, x_words, x_scales, w1, gs, offs, cand,
 
         def cast_weights(copy, h, g):
             copy(
-                w_bf[g][:, :, HALF * h : HALF * (h + 1), :].rearrange("p t m j -> p m j t"),
+                w_bf[g][:, :, HALF * h : HALF * (h + 1), :].rearrange("p u m j -> p m j u"),
                 w_raw[h][:].rearrange("p j (m t) -> p m j t", t=PACK)[:, :, :, 2 * g : 2 * g + 2],
             )
 
@@ -80,16 +88,17 @@ def tile_picked_candmed_none_p_kernel(tc, x_words, x_scales, w1, gs, offs, cand,
         cast_weights(nc.scalar.copy, 0, 0)
         cast_weights(nc.scalar.copy, 1, 0)
         cast_weights(nc.vector.tensor_copy, 1, 1)
-        for g in (1, 0):
+        pair_order = (1, 0)
+        for g in pair_order:
             cols = slice(2 * P * g, 2 * P * (g + 1))
             nc.vector.quantize_mx(
-                out=wq_w[:, cols].bitcast(FP8X4), scales=wq_s[:, cols], in_=w_bf[g][:].rearrange("p t m j -> p (t m j)")
+                out=wq_w[:, cols].bitcast(FP8X4), scales=wq_s[:, cols], in_=w_bf[g][:].rearrange("p u m j -> p (u m j)")
             )
 
         xc_s_by_t = placed_s[:, S : S + C].rearrange("p (m t) -> p t m", t=PACK)
         xc_s_first = held.tile([P, P], U8, name="xc_s_first", tag="w_bf0", align_bytes=64)
         nc.vector.tensor_copy(xc_s_first[:], xc_s_by_t[:, 0, :])
-        xc_w_first = held.tile([P, P], U32, name="xc_w_first", tag="w_bf1", align_bytes=64)
+        xc_w_first = held.tile([P, P], U32, name="xc_w_first", tag="w_raw1", align_bytes=64)
         nc.vector.tensor_copy(xc_w_first[:], xc_w_by_t[:, :, 0])
 
         zq_w = held.tile([P, S], U32, name="zq_w", align_bytes=64)
@@ -99,12 +108,12 @@ def tile_picked_candmed_none_p_kernel(tc, x_words, x_scales, w1, gs, offs, cand,
             held.tile([P, hi - lo, PACK], BF16, name="z_bf%d" % i, tag="z_bf%d" % i, align_bytes=64)
             for i, (lo, hi) in enumerate(z_spans)
         ]
-        z_bf = [z_tiles[0][:, 0:BLK, :], z_tiles[0][:, BLK : 2 * BLK, :], z_tiles[1][:], z_tiles[2][:]]
+        z_blocks = [z_tiles[0][:, 0:BLK, :], z_tiles[0][:, BLK : 2 * BLK, :], z_tiles[1][:], z_tiles[2][:]]
 
-        def first_product(u):
-            cols = slice(BLK * u, BLK * (u + 1))
-            h_ps = psum.tile([P, PACK, BLK], F32, name="h_ps", tag="bank%d" % u)
-            for t in (2, 3, 0, 1):
+        def first_product(b):
+            cols = slice(BLK * b, BLK * (b + 1))
+            h_ps = psum.tile([P, PACK, BLK], F32, name="h_ps", tag="bank%d" % b)
+            for t in [2 * g + u for g in pair_order for u in range(2)]:
                 feats = slice(P * t, P * (t + 1))
                 nc.tensor.matmul_mx(
                     out=h_ps[:, t, :],
@@ -116,7 +125,7 @@ def tile_picked_candmed_none_p_kernel(tc, x_words, x_scales, w1, gs, offs, cand,
                     stop=True,
                 )
             nc.vector.scalar_tensor_tensor(
-                out=z_bf[u],
+                out=z_blocks[b],
                 in0=h_ps[:].rearrange("p t n -> p n t"),
                 scalar=0.0,
                 in1=gs_t[:].to_broadcast([P, BLK, PACK]),
@@ -133,7 +142,8 @@ def tile_picked_candmed_none_p_kernel(tc, x_words, x_scales, w1, gs, offs, cand,
         window = [held.tile([P, 2 * S], F32, name="window%d" % t) for t in range(PACK)]
         own = [held.tile([P, S], F32, name="own%d" % t) for t in range(PACK)]
 
-        def second_product(t, lo, hi, bank, words, scales):
+        def second_product(t, span, bank, words, scales):
+            lo, hi = span
             s_ps = psum.tile([P, hi - lo], F32, name="s_ps", tag="bank%d" % bank)
             nc.tensor.matmul_mx(
                 out=s_ps[:],
@@ -144,63 +154,61 @@ def tile_picked_candmed_none_p_kernel(tc, x_words, x_scales, w1, gs, offs, cand,
                 start=True,
                 stop=True,
             )
-            nc.scalar.activation(window[t][:, lo:hi], s_ps[:], ACT.Copy, scale=-0.0625)
+            nc.scalar.activation(window[t][:, lo:hi], s_ps[:], ACT.Copy, scale=NEG_SIXTEENTH)
             return s_ps
 
-        def own_copy(t, lo, hi, s_ps):
-            nc.scalar.activation(own[t][:, lo:hi], s_ps[:], ACT.Copy, scale=-0.0625)
+        def own_copy(t, span, s_ps):
+            lo, hi = span
+            nc.scalar.activation(own[t][:, lo:hi], s_ps[:], ACT.Copy, scale=NEG_SIXTEENTH)
 
         first_product(0)
         first_product(1)
         first_product(2)
         quantise_z(0)
-        own_copy(0, 0, 2 * BLK, second_product(0, 0, 2 * BLK, 4, xc_w_first[:], xc_s_first[:]))
+        own_copy(0, z_spans[0], second_product(0, z_spans[0], PACK, xc_w_first[:], xc_s_first[:]))
         first_product(3)
         quantise_z(1)
-        third = second_product(0, 2 * BLK, 3 * BLK, 0, xc_w_first[:], xc_s_first[:])
+        span1_ps = second_product(0, z_spans[1], 0, xc_w_first[:], xc_s_first[:])
         quantise_z(2)
-        fourth = second_product(0, 3 * BLK, S, 1, xc_w_first[:], xc_s_first[:])
-        own_copy(0, 2 * BLK, 3 * BLK, third)
-        own_copy(0, 3 * BLK, S, fourth)
+        span2_ps = second_product(0, z_spans[2], 1, xc_w_first[:], xc_s_first[:])
+        own_copy(0, z_spans[1], span1_ps)
+        own_copy(0, z_spans[2], span2_ps)
+
         xc_s_rest = held.tile([P, PACK - 1, P], U8, name="xc_s_rest", tag="z_bf1", align_bytes=64)
         nc.vector.tensor_copy(xc_s_rest[:], xc_s_by_t[:, 1:PACK, :])
         xc_w_rest = held.tile([P, PACK - 1, P], U32, name="xc_w_rest", tag="z_bf2", align_bytes=64)
         nc.vector.tensor_copy(xc_w_rest[:].rearrange("p t m -> p m t"), xc_w_by_t[:, :, 1:PACK])
         for t in range(1, PACK):
-            own_copy(t, 0, S, second_product(t, 0, S, 4 + t, xc_w_rest[:, t - 1, :], xc_s_rest[:, t - 1, :]))
+            s_ps = second_product(t, (0, S), PACK + t, xc_w_rest[:, t - 1, :], xc_s_rest[:, t - 1, :])
+            own_copy(t, (0, S), s_ps)
 
-        da = [held.tile([P, S], F32, name="da%d" % t) for t in range(PACK)]
-        db = [held.tile([P, S], F32, name="db%d" % t) for t in range(PACK)]
-        low = [held.tile([P, S], F32, name="low%d" % t) for t in range(PACK)]
-        res = [held.tile([P, S], F32, name="res%d" % t) for t in range(PACK)]
         out_view = out.rearrange("(p t) j -> p t j", t=PACK)
-
-        def fetch(dst, lists, t, cols):
-            offsets = lists[:, cols.start // 16 : cols.stop // 16]
-            nc.vector.tensor_tensor(dst[t][:, cols], window[t][:].indirect(offsets), own[t][:, cols], ALU.subtract)
-
-        def clamp_low(t, cols):
-            nc.vector.scalar_tensor_tensor(
-                out=low[t][:, cols], in0=db[t][:, cols], scalar=0.0, in1=da[t][:, cols], op0=ALU.min, op1=ALU.max
-            )
-
-        def clamp_high(t, cols):
-            nc.vector.scalar_tensor_tensor(
-                out=res[t][:, cols], in0=db[t][:, cols], scalar=0.0, in1=low[t][:, cols], op0=ALU.max, op1=ALU.min
-            )
-            if t == PACK - 1:
-                nc.sync.dma_start(out_view[:, t, cols], res[t][:, cols])
-
         whole = slice(0, S)
         halves = [slice(0, S // 2), slice(S // 2, S)]
-        for t in range(PACK):
-            for cols in halves if t == 0 else [whole]:
-                fetch(da, n1_t, t, cols)
+
+        def fetch(dst, lists, t, cols):
+            offsets = lists[:, cols.start // GROUP : cols.stop // GROUP]
+            nc.vector.tensor_tensor(dst, window[t][:].indirect(offsets), own[t][:, cols], ALU.subtract)
+
+        for t0, t1 in ((0, PACK - 1), (PACK - 1, PACK)):
+            da = held.tile([P, t1 - t0, S], F32, name="da%d" % t0)
+            db = held.tile([P, t1 - t0, S], F32, name="db%d" % t0)
+            low = held.tile([P, t1 - t0, S], F32, name="low%d" % t0)
+            res = held.tile([P, t1 - t0, S], F32, name="res%d" % t0)
+            for t in range(t0, t1):
+                for cols in halves if t == 0 else [whole]:
+                    fetch(da[:, t - t0, cols], n1_t, t, cols)
+                for cols in halves if t == t1 - 1 else [whole]:
+                    fetch(db[:, t - t0, cols], n2_t, t, cols)
             for cols in halves:
-                fetch(db, n2_t, t, cols)
+                nc.vector.scalar_tensor_tensor(
+                    out=low[:, :, cols], in0=db[:, :, cols], scalar=0.0, in1=da[:, :, cols], op0=ALU.min, op1=ALU.max
+                )
             for cols in halves:
-                clamp_low(t, cols)
-            for cols in halves:
-                clamp_high(t, cols)
-            if t < PACK - 1:
-                nc.sync.dma_start(out_view[:, t, :], res[t][:])
+                nc.vector.scalar_tensor_tensor(
+                    out=res[:, :, cols], in0=db[:, :, cols], scalar=0.0, in1=low[:, :, cols], op0=ALU.max, op1=ALU.min
+                )
+                if t1 == PACK:
+                    nc.sync.dma_start(out_view[:, t0:t1, cols], res[:, :, cols])
+            if t1 < PACK:
+                nc.sync.dma_start(out_view[:, t0:t1, :], res[:])

from contextlib import ExitStack

import concourse.mybir as mybir

K, T, S, H, C = 512, 2048, 512, 512, 512
FLOPS = 2 * K * H * S + 2 * K * C * S

F32 = mybir.dt.float32
BF16 = mybir.dt.bfloat16
I32 = mybir.dt.int32
U32 = mybir.dt.uint32
U16 = mybir.dt.uint16
U8 = mybir.dt.uint8
FP8X4 = mybir.dt.float8_e4m3fn_x4
ALU = mybir.AluOpType
ACT = mybir.ActivationFunctionType

P = 128
PACK = 4
GROUP = 16
QUADRANT = 32
SCALE_ROWS = K // 32
BLK = 128
HALF = P // 2
NEG_SIXTEENTH = -0.0625


def tile_picked_candmed_none_p_kernel(tc, x_words, x_scales, w1, gs, offs, cand, n1, n2, out):
    nc = tc.nc
    with ExitStack() as ctx:
        held = ctx.enter_context(tc.tile_pool(name="held", bufs=1))
        psum = ctx.enter_context(tc.psum_pool(name="psum", bufs=1))

        offs_t = held.tile([P, S // GROUP], U16, name="offs_t")
        cand_t = held.tile([P, C // GROUP], U16, name="cand_t")
        n1_t = held.tile([P, S // GROUP], U16, name="n1_t")
        n2_t = held.tile([P, S // GROUP], U16, name="n2_t")
        xw = held.tile([P, T], I32, name="xw", align_bytes=64)
        xs = held.tile([P, T], U8, name="xs", align_bytes=64)
        gs_t = held.tile([P, 1, PACK], F32, name="gs_t")
        w_raw = [
            held.tile([P, PACK, H // 2], F32, name="w_raw%d" % h, tag="w_raw%d" % h, align_bytes=64) for h in range(2)
        ]

        for lo, hi in ((0, SCALE_ROWS), (QUADRANT, 2 * QUADRANT), (2 * QUADRANT, P)):
            nc.vector.memset(xs[lo:hi, :].bitcast(I32), 0)
        nc.sync.dma_start(offs_t[:], offs)
        nc.sync.dma_start(xs[SCALE_ROWS:QUADRANT, :].bitcast(I32), x_scales[0].bitcast(I32))
        nc.sync.dma_start(cand_t[:], cand)
        nc.scalar.dma_start(gs_t[:], gs.rearrange("(p t) o -> p o t", t=PACK))
        nc.sync.dma_start(xw[:], x_words[0].rearrange("p n t -> p (n t)").bitcast(I32))
        w_view = w1.rearrange("(p j) c -> p j c", j=PACK)
        for h in range(2):
            nc.sync.dma_start(w_raw[h][:], w_view[:, :, h * (H // 2) : (h + 1) * (H // 2)])
        nc.sync.dma_start(n1_t[:], n1)
        nc.sync.dma_start(n2_t[:], n2)

        xq_w = held.tile([P, S], U32, name="xq_w", align_bytes=64)
        picked_s = held.tile([P, S + C], U8, name="picked_s", align_bytes=64)
        placed_s = held.tile([P, S + C], U8, name="placed_s", align_bytes=64)
        nc.vector.memset(placed_s[:].bitcast(I32), 0)
        xc_w_list = held.tile([P, C], U32, name="xc_w_list", align_bytes=64)

        nc.vector.tensor_copy(picked_s[:, 0:S], xs[:].indirect(offs_t[:]))
        nc.vector.tensor_copy(picked_s[:, S : S + C], xs[:].indirect(cand_t[:]))
        for q in range(P // QUADRANT):
            nc.sync.dma_start(
                placed_s[QUADRANT * q : QUADRANT * q + PACK, :].bitcast(I32),
                picked_s[SCALE_ROWS + PACK * q : SCALE_ROWS + PACK * (q + 1), :].bitcast(I32),
            )
        nc.vector.tensor_copy(xq_w[:], xw[:].bitcast(U32).indirect(offs_t[:]))
        nc.vector.tensor_copy(xc_w_list[:], xw[:].bitcast(U32).indirect(cand_t[:]))
        xc_w_by_t = xc_w_list[:].rearrange("p (m t) -> p m t", t=PACK)

        wq_w = held.tile([P, H], U32, name="wq_w", align_bytes=64)
        wq_s = held.tile([P, H], U8, name="wq_s", align_bytes=64)
        w_bf = [
            held.tile([P, 2, P, PACK], BF16, name="w_bf%d" % g, tag="w_bf%d" % g, align_bytes=64) for g in range(2)
        ]

        def cast_weights(copy, h, g):
            copy(
                w_bf[g][:, :, HALF * h : HALF * (h + 1), :].rearrange("p u m j -> p m j u"),
                w_raw[h][:].rearrange("p j (m t) -> p m j t", t=PACK)[:, :, :, 2 * g : 2 * g + 2],
            )

        cast_weights(nc.scalar.copy, 0, 1)
        cast_weights(nc.scalar.copy, 0, 0)
        cast_weights(nc.scalar.copy, 1, 0)
        cast_weights(nc.vector.tensor_copy, 1, 1)
        pair_order = (1, 0)
        for g in pair_order:
            cols = slice(2 * P * g, 2 * P * (g + 1))
            nc.vector.quantize_mx(
                out=wq_w[:, cols].bitcast(FP8X4), scales=wq_s[:, cols], in_=w_bf[g][:].rearrange("p u m j -> p (u m j)")
            )

        xc_s_by_t = placed_s[:, S : S + C].rearrange("p (m t) -> p t m", t=PACK)
        xc_s_first = held.tile([P, P], U8, name="xc_s_first", tag="w_bf0", align_bytes=64)
        nc.vector.tensor_copy(xc_s_first[:], xc_s_by_t[:, 0, :])
        xc_w_first = held.tile([P, P], U32, name="xc_w_first", tag="w_raw1", align_bytes=64)
        nc.vector.tensor_copy(xc_w_first[:], xc_w_by_t[:, :, 0])

        zq_w = held.tile([P, S], U32, name="zq_w", align_bytes=64)
        zq_s = held.tile([P, S], U8, name="zq_s", align_bytes=64)
        z_spans = [(0, 2 * BLK), (2 * BLK, 3 * BLK), (3 * BLK, S)]
        z_tiles = [
            held.tile([P, hi - lo, PACK], BF16, name="z_bf%d" % i, tag="z_bf%d" % i, align_bytes=64)
            for i, (lo, hi) in enumerate(z_spans)
        ]
        z_blocks = [z_tiles[0][:, 0:BLK, :], z_tiles[0][:, BLK : 2 * BLK, :], z_tiles[1][:], z_tiles[2][:]]

        def first_product(b):
            cols = slice(BLK * b, BLK * (b + 1))
            h_ps = psum.tile([P, PACK, BLK], F32, name="h_ps", tag="bank%d" % b)
            for t in [2 * g + u for g in pair_order for u in range(2)]:
                feats = slice(P * t, P * (t + 1))
                nc.tensor.matmul_mx(
                    out=h_ps[:, t, :],
                    lhsT=wq_w[:, feats].bitcast(FP8X4),
                    lhsT_scale=wq_s[:, feats],
                    rhs=xq_w[:, cols].bitcast(FP8X4),
                    rhs_scale=placed_s[:, cols],
                    start=True,
                    stop=True,
                )
            nc.vector.scalar_tensor_tensor(
                out=z_blocks[b],
                in0=h_ps[:].rearrange("p t n -> p n t"),
                scalar=0.0,
                in1=gs_t[:].to_broadcast([P, BLK, PACK]),
                op0=ALU.max,
                op1=ALU.mult,
            )

        def quantise_z(i):
            cols = slice(*z_spans[i])
            nc.vector.quantize_mx(
                out=zq_w[:, cols].bitcast(FP8X4), scales=zq_s[:, cols], in_=z_tiles[i][:].rearrange("p n t -> p (n t)")
            )

        window = [held.tile([P, 2 * S], F32, name="window%d" % t) for t in range(PACK)]
        own = [held.tile([P, S], F32, name="own%d" % t) for t in range(PACK)]

        def second_product(t, span, bank, words, scales):
            lo, hi = span
            s_ps = psum.tile([P, hi - lo], F32, name="s_ps", tag="bank%d" % bank)
            nc.tensor.matmul_mx(
                out=s_ps[:],
                lhsT=words.bitcast(FP8X4),
                lhsT_scale=scales,
                rhs=zq_w[:, lo:hi].bitcast(FP8X4),
                rhs_scale=zq_s[:, lo:hi],
                start=True,
                stop=True,
            )
            nc.scalar.activation(window[t][:, lo:hi], s_ps[:], ACT.Copy, scale=NEG_SIXTEENTH)
            return s_ps

        def own_copy(t, span, s_ps):
            lo, hi = span
            nc.scalar.activation(own[t][:, lo:hi], s_ps[:], ACT.Copy, scale=NEG_SIXTEENTH)

        first_product(0)
        first_product(1)
        first_product(2)
        quantise_z(0)
        own_copy(0, z_spans[0], second_product(0, z_spans[0], PACK, xc_w_first[:], xc_s_first[:]))
        first_product(3)
        quantise_z(1)
        span1_ps = second_product(0, z_spans[1], 0, xc_w_first[:], xc_s_first[:])
        quantise_z(2)
        span2_ps = second_product(0, z_spans[2], 1, xc_w_first[:], xc_s_first[:])
        own_copy(0, z_spans[1], span1_ps)
        own_copy(0, z_spans[2], span2_ps)

        xc_s_rest = held.tile([P, PACK - 1, P], U8, name="xc_s_rest", tag="z_bf1", align_bytes=64)
        nc.vector.tensor_copy(xc_s_rest[:], xc_s_by_t[:, 1:PACK, :])
        xc_w_rest = held.tile([P, PACK - 1, P], U32, name="xc_w_rest", tag="z_bf2", align_bytes=64)
        nc.vector.tensor_copy(xc_w_rest[:].rearrange("p t m -> p m t"), xc_w_by_t[:, :, 1:PACK])
        for t in range(1, PACK):
            s_ps = second_product(t, (0, S), PACK + t, xc_w_rest[:, t - 1, :], xc_s_rest[:, t - 1, :])
            own_copy(t, (0, S), s_ps)

        out_view = out.rearrange("(p t) j -> p t j", t=PACK)
        whole = slice(0, S)
        halves = [slice(0, S // 2), slice(S // 2, S)]

        def fetch(dst, lists, t, cols):
            offsets = lists[:, cols.start // GROUP : cols.stop // GROUP]
            nc.vector.tensor_tensor(dst, window[t][:].indirect(offsets), own[t][:, cols], ALU.subtract)

        for t0, t1 in ((0, PACK - 1), (PACK - 1, PACK)):
            da = held.tile([P, t1 - t0, S], F32, name="da%d" % t0)
            db = held.tile([P, t1 - t0, S], F32, name="db%d" % t0)
            low = held.tile([P, t1 - t0, S], F32, name="low%d" % t0)
            res = held.tile([P, t1 - t0, S], F32, name="res%d" % t0)
            for t in range(t0, t1):
                for cols in halves if t == 0 else [whole]:
                    fetch(da[:, t - t0, cols], n1_t, t, cols)
                for cols in halves if t == t1 - 1 else [whole]:
                    fetch(db[:, t - t0, cols], n2_t, t, cols)
            for cols in halves:
                nc.vector.scalar_tensor_tensor(
                    out=low[:, :, cols], in0=db[:, :, cols], scalar=0.0, in1=da[:, :, cols], op0=ALU.min, op1=ALU.max
                )
            for cols in halves:
                nc.vector.scalar_tensor_tensor(
                    out=res[:, :, cols], in0=db[:, :, cols], scalar=0.0, in1=low[:, :, cols], op0=ALU.max, op1=ALU.min
                )
                if t1 == PACK:
                    nc.sync.dma_start(out_view[:, t0:t1, cols], res[:, :, cols])
            if t1 < PACK:
                nc.sync.dma_start(out_view[:, t0:t1, :], res[:])
